import numpy as np
import ml_dtypes


def mxq(x, axis, fmt="e4m3"):
    dtype, down = {"e4m3": (ml_dtypes.float8_e4m3fn, 7), "e5m2": (ml_dtypes.float8_e5m2, 14)}[fmt]
    v = np.moveaxis(np.asarray(x, np.float32).astype(ml_dtypes.bfloat16).astype(np.float64), axis, -1)
    blocks = v.reshape(v.shape[:-1] + (-1, 32))
    amax = np.abs(blocks).max(-1, keepdims=True)
    byte = np.maximum(np.where(amax > 0, np.frexp(amax)[1] - 1 + 127, 0) - down, 1)
    scale = np.exp2(byte - 127.0)
    codes = (blocks / scale).astype(np.float32).astype(dtype).astype(np.float64)
    return np.moveaxis((codes * scale).reshape(v.shape), -1, axis)


WIDE = False


def mx_kscale(k):
    if not WIDE:
        return np.ones(k)
    levels = np.array([30, -30])
    if k % 512:
        return np.exp2(np.random.permutation(np.resize(levels, k // 32))).repeat(32)
    a = np.empty((k // 512, 16))
    for p in range(k // 512):
        a[p, :8] = np.random.permutation(np.resize(levels, 8))
        for g in range(8):
            far = levels[np.abs(levels - a[p, g]) >= 10]
            a[p, g + 8] = far[np.random.randint(len(far))]
    return np.exp2(a.ravel()).repeat(32)


def f64(x):
    return np.asarray(x).astype(np.float64)


E2M1 = np.array([0.0, 0.5, 1.0, 1.5, 2.0, 3.0, 4.0, 6.0, -0.0, -0.5, -1.0, -1.5, -2.0, -3.0, -4.0, -6.0])


def pack_weight(w, fmt):
    k, n = w.shape
    w = f64(np.asarray(w, np.float32).astype(ml_dtypes.bfloat16)).reshape(k // 32, 32, n)
    amax = np.abs(w).max(1)
    if fmt == "e4m3":
        byte = np.frexp(amax)[1] - 1 + 127 - 7
    else:
        mant, ex = np.frexp(amax / 6.0)
        byte = np.where(mant > 0.5, ex, ex - 1) + 127
    byte = np.clip(np.where(amax > 0, byte, 1), 1, 254)
    scaled = (w * np.exp2(127.0 - byte)[:, None, :]).reshape(k, n).astype(np.float32)
    by_word = np.ascontiguousarray(scaled.reshape(k // 512, 128, 4, n).transpose(0, 1, 3, 2))
    if fmt == "e4m3":
        words = by_word.astype(ml_dtypes.float8_e4m3fn).view(np.uint8)
    else:
        c = by_word.astype(ml_dtypes.float4_e2m1fn).view(np.uint8) & 0xF
        words = (c[..., 0::2] | (c[..., 1::2] << 4)).reshape(k // 512, 128, 2 * n)
    return np.ascontiguousarray(words), np.ascontiguousarray(byte.astype(np.uint8).reshape(k // 512, 16, n))


def unpack_weight(words, scales, fmt):
    g, _, n = scales.shape
    words = np.ascontiguousarray(words).reshape(g, 128, n, -1)
    if fmt == "e4m3":
        vals = words.view(ml_dtypes.float8_e4m3fn).astype(np.float64)
    else:
        nib = np.empty((g, 128, n, 4), np.uint8)
        nib[..., 0::2] = words & 0xF
        nib[..., 1::2] = words >> 4
        vals = E2M1[nib]
    vals = vals * np.repeat(np.exp2(scales.astype(np.float64) - 127.0), 8, axis=1)[..., None]
    return vals.transpose(0, 1, 3, 2).reshape(g * 512, n)


O, T, D, H = 1024, 1536, 256, 1536


def setup_inputs():
    n = np.random.standard_normal
    s = mx_kscale(T)[:, None]
    m = np.exp(0.5 * n((T, 1)))
    x = n((T, D)) * s
    p_x4 = pack_weight(x[:O], "e2m1")
    return {
        "x4_words": p_x4[0],
        "x4_scales": p_x4[1],
        "x8": (x[O:]).astype(np.float32),
        "dy": (m * n((T, H)) / np.sqrt(T) / s).astype(np.float32),
        "w": (0.1 * n((256, 1536))).astype(np.float32),
    }


def reference(x4_words, x4_scales, x8, dy, w):
    x4_ = unpack_weight(x4_words, x4_scales, "e2m1")
    x8_ = mxq(f64(x8), 0, "e4m3")
    dy_ = mxq(f64(dy), 0, "e5m2")
    y = x4_.T @ dy_[:O] + x8_.T @ dy_[O:]
    return f64(w) - 0.0625 * y

@@ -1,0 +1,140 @@
+from contextlib import ExitStack
+
+import concourse.mybir as mybir
+
+FLOPS = 2 * 1536 * 256 * 1536
+
+F32 = mybir.dt.float32
+BF16 = mybir.dt.bfloat16
+I32 = mybir.dt.int32
+U32 = mybir.dt.uint32
+U8 = mybir.dt.uint8
+E4M3 = mybir.dt.float8_e4m3fn_x4
+E5M2 = mybir.dt.float8_e5m2_x4
+E2M1 = mybir.dt.float4_e2m1fn_x4
+MULT = mybir.AluOpType.mult
+ADD = mybir.AluOpType.add
+
+P = 128
+N = 512
+T, D, H = 1536, 256, 1536
+
+
+def tile_mix_dwsav_sgd_kernel(tc, x4_words, x4_scales, x8, dy, w, out):
+    nc = tc.nc
+    with ExitStack() as ctx:
+        pool = ctx.enter_context(tc.tile_pool(name="pool", bufs=1))
+        psum = ctx.enter_context(tc.psum_pool(name="psum", bufs=1))
+        ctx.enter_context(tc.manual_schedule())
+
+        acc = {}
+        for c in range(3):
+            for m in range(2):
+                acc[c, m] = psum.tile([P, N], F32, name="acc_%d_%d" % (c, m))
+
+        def load_dy(g, lo, hi):
+            raw = pool.tile([P, 4, hi - lo], F32, name="raw_%d_%d" % (g, lo), align_bytes=64)
+            rows = dy[512 * g : 512 * (g + 1), lo:hi]
+            nc.sync.dma_start(out=raw[:], in_=rows.rearrange("(p j) h -> p j h", j=4))
+            return raw
+
+        def load_w(c):
+            t = pool.tile([P, 2, N], F32, name="w_%d" % c, align_bytes=64)
+            nc.sync.dma_start(out=t[:], in_=w[:, N * c : N * (c + 1)].rearrange("(m p) h -> p m h", m=2))
+            return t
+
+        x4_sc = pool.tile([P, 2, D], U8, name="x4_sc", align_bytes=64)
+        nc.vector.memset(x4_sc[:].rearrange("p a n -> p (a n)").bitcast(I32), 0)
+
+        x8_raw = pool.tile([P, 4, D], F32, name="x8_raw", align_bytes=64)
+        nc.sync.dma_start(out=x8_raw[:], in_=x8.rearrange("(p j) d -> p j d", j=4))
+        x4_wd = pool.tile([P, 2, 2 * D], U8, name="x4_wd", align_bytes=64)
+        nc.sync.dma_start(out=x4_wd[:].bitcast(I32), in_=x4_words.rearrange("a p b -> p a b").bitcast(I32))
+        raw2 = load_dy(2, 0, H)
+        for q in range(4):
+            nc.scalar.dma_start(
+                out=x4_sc[32 * q : 32 * q + 4, :, :].bitcast(I32),
+                in_=x4_scales[:, 4 * q : 4 * q + 4, :].rearrange("a r n -> r a n").bitcast(I32),
+            )
+        raw0 = load_dy(0, 0, H)
+        raw1a = load_dy(1, 0, 2 * N)
+        w_sb = [load_w(0)]
+        raw1b = load_dy(1, 2 * N, H)
+        w_sb.append(load_w(1))
+        w_sb.append(load_w(2))
+
+        grouped, codes, scales = {}, {}, {}
+
+        def interleave(g, c, raw, col, v):
+            t = pool.tile([P, N, 4], BF16, name="grp_%d_%d" % (g, c), align_bytes=64)
+            grouped[g, c] = t
+            nc.scalar.copy(out=t[:, v:N, :], in_=raw[:, :, col + v : col + N].rearrange("p j h -> p h j"))
+            nc.vector.tensor_copy(out=t[:, 0:v, :], in_=raw[:, :, col : col + v].rearrange("p j h -> p h j"))
+
+        def quantize(g, c):
+            k = pool.tile([P, N], U32, name="cod_%d_%d" % (g, c), align_bytes=64)
+            s = pool.tile([P, N], U8, name="sca_%d_%d" % (g, c), align_bytes=64)
+            nc.vector.quantize_mx(
+                out=k[:].bitcast(E5M2), scales=s[:], in_=grouped[g, c][:].rearrange("p h j -> p (h j)")
+            )
+            codes[g, c], scales[g, c] = k, s
+
+        def multiply(g, c, start, stop):
+            for m in range(2):
+                if g == 2:
+                    lhsT = x8_codes[:, P * m : P * (m + 1)].bitcast(E4M3)
+                    lhsT_scale = x8_scales[:, P * m : P * (m + 1)]
+                else:
+                    lhsT = x4_wd[:, g, 2 * P * m : 2 * P * (m + 1)].bitcast(E2M1)
+                    lhsT_scale = x4_sc[:, g, P * m : P * (m + 1)]
+                nc.tensor.matmul_mx(
+                    out=acc[c, m][:],
+                    lhsT=lhsT,
+                    lhsT_scale=lhsT_scale,
+                    rhs=codes[g, c][:].bitcast(E5M2),
+                    rhs_scale=scales[g, c][:],
+                    start=start,
+                    stop=stop,
+                )
+
+        def finish(c, m):
+            o = pool.tile([P, N], F32, name="o_%d_%d" % (c, m), align_bytes=64)
+            nc.vector.scalar_tensor_tensor(
+                out=o[:], in0=acc[c, m][:], scalar=-0.0625, in1=w_sb[c][:, m, :], op0=MULT, op1=ADD
+            )
+            nc.sync.dma_start(out=out[P * m : P * (m + 1), N * c : N * (c + 1)], in_=o[:])
+
+        x8_grp = pool.tile([P, D, 4], BF16, name="x8_grp", align_bytes=64)
+        nc.scalar.copy(out=x8_grp[:], in_=x8_raw[:].rearrange("p j d -> p d j"))
+        x8_codes = pool.tile([P, D], U32, name="x8_codes", align_bytes=64)
+        x8_scales = pool.tile([P, D], U8, name="x8_scales", align_bytes=64)
+        nc.vector.quantize_mx(
+            out=x8_codes[:].bitcast(E4M3), scales=x8_scales[:], in_=x8_grp[:].rearrange("p d j -> p (d j)")
+        )
+
+        for g, raw, start in ((2, raw2, True), (0, raw0, False)):
+            interleave(g, 0, raw, 0, 256)
+            interleave(g, 1, raw, N, 256)
+            quantize(g, 0)
+            multiply(g, 0, start, False)
+            interleave(g, 2, raw, 2 * N, 256)
+            quantize(g, 1)
+            multiply(g, 1, start, False)
+            quantize(g, 2)
+            multiply(g, 2, start, False)
+
+        interleave(1, 0, raw1a, 0, 160)
+        interleave(1, 1, raw1a, N, 160)
+        quantize(1, 0)
+        multiply(1, 0, False, True)
+        quantize(1, 1)
+        multiply(1, 1, False, True)
+        finish(0, 0)
+        interleave(1, 2, raw1b, 0, 320)
+        finish(0, 1)
+        quantize(1, 2)
+        multiply(1, 2, False, True)
+        finish(1, 0)
+        finish(1, 1)
+        finish(2, 0)
+        finish(2, 1)

@@ -38,11 +38,6 @@ def tile_mix_dwsav_sgd_kernel(tc, x4_words, x4_scales, x8, dy, w, out):
             nc.sync.dma_start(out=raw[:], in_=rows.rearrange("(p j) h -> p j h", j=4))
             return raw
 
-        def load_w(c):
-            t = pool.tile([P, 2, N], F32, name="w_%d" % c, align_bytes=64)
-            nc.sync.dma_start(out=t[:], in_=w[:, N * c : N * (c + 1)].rearrange("(m p) h -> p m h", m=2))
-            return t
-
         x4_sc = pool.tile([P, 2, D], U8, name="x4_sc", align_bytes=64)
         nc.vector.memset(x4_sc[:].rearrange("p a n -> p (a n)").bitcast(I32), 0)
 
@@ -58,18 +53,28 @@ def tile_mix_dwsav_sgd_kernel(tc, x4_words, x4_scales, x8, dy, w, out):
             )
         raw0 = load_dy(0, 0, H)
         raw1a = load_dy(1, 0, 2 * N)
-        w_sb = [load_w(0)]
+        w_a = pool.tile([P, 2, N], F32, name="w_a", align_bytes=64)
+        nc.sync.dma_start(out=w_a[:], in_=w[:, 0:N].rearrange("(m p) h -> p m h", m=2))
         raw1b = load_dy(1, 2 * N, H)
-        w_sb.append(load_w(1))
-        w_sb.append(load_w(2))
+        w_b = []
+        for m in range(2):
+            t = pool.tile([P, 2 * N], F32, name="w_b%d" % m, align_bytes=64)
+            nc.sync.dma_start(out=t[:], in_=w[P * m : P * (m + 1), N:H])
+            w_b.append(t)
 
         grouped, codes, scales = {}, {}, {}
 
         def interleave(g, c, raw, col, v):
             t = pool.tile([P, N, 4], BF16, name="grp_%d_%d" % (g, c), align_bytes=64)
             grouped[g, c] = t
-            nc.scalar.copy(out=t[:, v:N, :], in_=raw[:, :, col + v : col + N].rearrange("p j h -> p h j"))
-            nc.vector.tensor_copy(out=t[:, 0:v, :], in_=raw[:, :, col : col + v].rearrange("p j h -> p h j"))
+            nc.scalar.copy(
+                out=t[:, v:N, :].rearrange("p (c i) j -> p c j i", i=4),
+                in_=raw[:, :, col + v : col + N].rearrange("p j (c i) -> p c j i", i=4),
+            )
+            nc.vector.tensor_copy(
+                out=t[:, 0:v, :].rearrange("p (c i) j -> p c j i", i=4),
+                in_=raw[:, :, col : col + v].rearrange("p j (c i) -> p c j i", i=4),
+            )
 
         def quantize(g, c):
             k = pool.tile([P, N], U32, name="cod_%d_%d" % (g, c), align_bytes=64)
@@ -99,9 +104,8 @@ def tile_mix_dwsav_sgd_kernel(tc, x4_words, x4_scales, x8, dy, w, out):
 
         def finish(c, m):
             o = pool.tile([P, N], F32, name="o_%d_%d" % (c, m), align_bytes=64)
-            nc.vector.scalar_tensor_tensor(
-                out=o[:], in0=acc[c, m][:], scalar=-0.0625, in1=w_sb[c][:, m, :], op0=MULT, op1=ADD
-            )
+            w_cm = w_a[:, m, :] if c == 0 else w_b[m][:, N * (c - 1) : N * c]
+            nc.vector.scalar_tensor_tensor(out=o[:], in0=acc[c, m][:], scalar=-0.0625, in1=w_cm, op0=MULT, op1=ADD)
             nc.sync.dma_start(out=out[P * m : P * (m + 1), N * c : N * (c + 1)], in_=o[:])
 
         x8_grp = pool.tile([P, D, 4], BF16, name="x8_grp", align_bytes=64)
@@ -135,6 +139,6 @@ def tile_mix_dwsav_sgd_kernel(tc, x4_words, x4_scales, x8, dy, w, out):
         quantize(1, 2)
         multiply(1, 2, False, True)
         finish(1, 0)
-        finish(1, 1)
         finish(2, 0)
+        finish(1, 1)
         finish(2, 1)

@@ -53,9 +53,9 @@ def tile_mix_dwsav_sgd_kernel(tc, x4_words, x4_scales, x8, dy, w, out):
             )
         raw0 = load_dy(0, 0, H)
         raw1a = load_dy(1, 0, 2 * N)
+        raw1b = load_dy(1, 2 * N, H)
         w_a = pool.tile([P, 2, N], F32, name="w_a", align_bytes=64)
         nc.sync.dma_start(out=w_a[:], in_=w[:, 0:N].rearrange("(m p) h -> p m h", m=2))
-        raw1b = load_dy(1, 2 * N, H)
         w_b = []
         for m in range(2):
             t = pool.tile([P, 2 * N], F32, name="w_b%d" % m, align_bytes=64)
@@ -102,11 +102,17 @@ def tile_mix_dwsav_sgd_kernel(tc, x4_words, x4_scales, x8, dy, w, out):
                     stop=stop,
                 )
 
-        def finish(c, m):
-            o = pool.tile([P, N], F32, name="o_%d_%d" % (c, m), align_bytes=64)
+        def finish(c, m, parts=1):
             w_cm = w_a[:, m, :] if c == 0 else w_b[m][:, N * (c - 1) : N * c]
-            nc.vector.scalar_tensor_tensor(out=o[:], in0=acc[c, m][:], scalar=-0.0625, in1=w_cm, op0=MULT, op1=ADD)
-            nc.sync.dma_start(out=out[P * m : P * (m + 1), N * c : N * (c + 1)], in_=o[:])
+            width = N // parts
+            for i in range(parts):
+                cols = slice(width * i, width * (i + 1))
+                o = pool.tile([P, width], F32, name="o_%d_%d_%d" % (c, m, i), align_bytes=64)
+                nc.vector.scalar_tensor_tensor(
+                    out=o[:], in0=acc[c, m][:, cols], scalar=-0.0625, in1=w_cm[:, cols], op0=MULT, op1=ADD
+                )
+                h0 = N * c + width * i
+                nc.sync.dma_start(out=out[P * m : P * (m + 1), h0 : h0 + width], in_=o[:])
 
         x8_grp = pool.tile([P, D, 4], BF16, name="x8_grp", align_bytes=64)
         nc.scalar.copy(out=x8_grp[:], in_=x8_raw[:].rearrange("p j d -> p d j"))
@@ -127,18 +133,18 @@ def tile_mix_dwsav_sgd_kernel(tc, x4_words, x4_scales, x8, dy, w, out):
             quantize(g, 2)
             multiply(g, 2, start, False)
 
-        interleave(1, 0, raw1a, 0, 160)
-        interleave(1, 1, raw1a, N, 160)
+        interleave(1, 0, raw1a, 0, 288)
+        interleave(1, 1, raw1a, N, 288)
         quantize(1, 0)
         multiply(1, 0, False, True)
         quantize(1, 1)
         multiply(1, 1, False, True)
-        finish(0, 0)
-        interleave(1, 2, raw1b, 0, 320)
-        finish(0, 1)
+        interleave(1, 2, raw1b, 0, 288)
         quantize(1, 2)
         multiply(1, 2, False, True)
+        finish(0, 0)
+        finish(0, 1)
         finish(1, 0)
         finish(2, 0)
         finish(1, 1)
-        finish(2, 1)
+        finish(2, 1, parts=2)

@@ -54,27 +54,27 @@ def tile_mix_dwsav_sgd_kernel(tc, x4_words, x4_scales, x8, dy, w, out):
         raw0 = load_dy(0, 0, H)
         raw1a = load_dy(1, 0, 2 * N)
         raw1b = load_dy(1, 2 * N, H)
-        w_a = pool.tile([P, 2, N], F32, name="w_a", align_bytes=64)
-        nc.sync.dma_start(out=w_a[:], in_=w[:, 0:N].rearrange("(m p) h -> p m h", m=2))
-        w_b = []
-        for m in range(2):
-            t = pool.tile([P, 2 * N], F32, name="w_b%d" % m, align_bytes=64)
-            nc.sync.dma_start(out=t[:], in_=w[P * m : P * (m + 1), N:H])
-            w_b.append(t)
+        w_sb = {}
+        for c in range(3):
+            for m in range(2):
+                w_sb[c, m] = pool.tile([P, N], F32, name="w_%d_%d" % (c, m), align_bytes=64)
+                nc.sync.dma_start(out=w_sb[c, m][:], in_=w[P * m : P * (m + 1), N * c : N * (c + 1)])
 
         grouped, codes, scales = {}, {}, {}
 
         def interleave(g, c, raw, col, v):
             t = pool.tile([P, N, 4], BF16, name="grp_%d_%d" % (g, c), align_bytes=64)
             grouped[g, c] = t
-            nc.scalar.copy(
-                out=t[:, v:N, :].rearrange("p (c i) j -> p c j i", i=4),
-                in_=raw[:, :, col + v : col + N].rearrange("p j (c i) -> p c j i", i=4),
-            )
-            nc.vector.tensor_copy(
-                out=t[:, 0:v, :].rearrange("p (c i) j -> p c j i", i=4),
-                in_=raw[:, :, col : col + v].rearrange("p j (c i) -> p c j i", i=4),
-            )
+            if v < N:
+                nc.scalar.copy(
+                    out=t[:, v:N, :].rearrange("p (c i) j -> p c j i", i=4),
+                    in_=raw[:, :, col + v : col + N].rearrange("p j (c i) -> p c j i", i=4),
+                )
+            if v > 0:
+                nc.vector.tensor_copy(
+                    out=t[:, 0:v, :].rearrange("p (c i) j -> p c j i", i=4),
+                    in_=raw[:, :, col : col + v].rearrange("p j (c i) -> p c j i", i=4),
+                )
 
         def quantize(g, c):
             k = pool.tile([P, N], U32, name="cod_%d_%d" % (g, c), align_bytes=64)
@@ -103,13 +103,12 @@ def tile_mix_dwsav_sgd_kernel(tc, x4_words, x4_scales, x8, dy, w, out):
                 )
 
         def finish(c, m, parts=1):
-            w_cm = w_a[:, m, :] if c == 0 else w_b[m][:, N * (c - 1) : N * c]
             width = N // parts
             for i in range(parts):
                 cols = slice(width * i, width * (i + 1))
                 o = pool.tile([P, width], F32, name="o_%d_%d_%d" % (c, m, i), align_bytes=64)
                 nc.vector.scalar_tensor_tensor(
-                    out=o[:], in0=acc[c, m][:, cols], scalar=-0.0625, in1=w_cm[:, cols], op0=MULT, op1=ADD
+                    out=o[:], in0=acc[c, m][:, cols], scalar=-0.0625, in1=w_sb[c, m][:, cols], op0=MULT, op1=ADD
                 )
                 h0 = N * c + width * i
                 nc.sync.dma_start(out=out[P * m : P * (m + 1), h0 : h0 + width], in_=o[:])
@@ -133,18 +132,18 @@ def tile_mix_dwsav_sgd_kernel(tc, x4_words, x4_scales, x8, dy, w, out):
             quantize(g, 2)
             multiply(g, 2, start, False)
 
-        interleave(1, 0, raw1a, 0, 288)
-        interleave(1, 1, raw1a, N, 288)
+        interleave(1, 0, raw1a, 0, 512)
+        interleave(1, 1, raw1a, N, 32)
         quantize(1, 0)
         multiply(1, 0, False, True)
         quantize(1, 1)
         multiply(1, 1, False, True)
-        interleave(1, 2, raw1b, 0, 288)
-        quantize(1, 2)
-        multiply(1, 2, False, True)
+        interleave(1, 2, raw1b, 0, 128)
         finish(0, 0)
         finish(0, 1)
+        quantize(1, 2)
+        multiply(1, 2, False, True)
         finish(1, 0)
-        finish(2, 0)
         finish(1, 1)
+        finish(2, 0)
         finish(2, 1, parts=2)

from contextlib import ExitStack

import concourse.mybir as mybir

FLOPS = 2 * 1536 * 256 * 1536

F32 = mybir.dt.float32
BF16 = mybir.dt.bfloat16
I32 = mybir.dt.int32
U32 = mybir.dt.uint32
U8 = mybir.dt.uint8
E4M3 = mybir.dt.float8_e4m3fn_x4
E5M2 = mybir.dt.float8_e5m2_x4
E2M1 = mybir.dt.float4_e2m1fn_x4
MULT = mybir.AluOpType.mult
ADD = mybir.AluOpType.add

P = 128
N = 512
T, D, H = 1536, 256, 1536


def tile_mix_dwsav_sgd_kernel(tc, x4_words, x4_scales, x8, dy, w, out):
    nc = tc.nc
    with ExitStack() as ctx:
        pool = ctx.enter_context(tc.tile_pool(name="pool", bufs=1))
        psum = ctx.enter_context(tc.psum_pool(name="psum", bufs=1))
        ctx.enter_context(tc.manual_schedule())

        acc = {}
        for c in range(3):
            for m in range(2):
                acc[c, m] = psum.tile([P, N], F32, name="acc_%d_%d" % (c, m))

        def load_dy(g, lo, hi):
            raw = pool.tile([P, 4, hi - lo], F32, name="raw_%d_%d" % (g, lo), align_bytes=64)
            rows = dy[512 * g : 512 * (g + 1), lo:hi]
            nc.sync.dma_start(out=raw[:], in_=rows.rearrange("(p j) h -> p j h", j=4))
            return raw

        x4_sc = pool.tile([P, 2, D], U8, name="x4_sc", align_bytes=64)
        nc.vector.memset(x4_sc[:].rearrange("p a n -> p (a n)").bitcast(I32), 0)

        x8_raw = pool.tile([P, 4, D], F32, name="x8_raw", align_bytes=64)
        nc.sync.dma_start(out=x8_raw[:], in_=x8.rearrange("(p j) d -> p j d", j=4))
        x4_wd = pool.tile([P, 2, 2 * D], U8, name="x4_wd", align_bytes=64)
        nc.sync.dma_start(out=x4_wd[:].bitcast(I32), in_=x4_words.rearrange("a p b -> p a b").bitcast(I32))
        raw2 = load_dy(2, 0, H)
        for q in range(4):
            nc.scalar.dma_start(
                out=x4_sc[32 * q : 32 * q + 4, :, :].bitcast(I32),
                in_=x4_scales[:, 4 * q : 4 * q + 4, :].rearrange("a r n -> r a n").bitcast(I32),
            )
        raw0 = load_dy(0, 0, H)
        raw1a = load_dy(1, 0, 2 * N)
        raw1b = load_dy(1, 2 * N, H)
        w_sb = {}
        for c in range(3):
            for m in range(2):
                w_sb[c, m] = pool.tile([P, N], F32, name="w_%d_%d" % (c, m), align_bytes=64)
                nc.sync.dma_start(out=w_sb[c, m][:], in_=w[P * m : P * (m + 1), N * c : N * (c + 1)])

        grouped, codes, scales = {}, {}, {}

        def interleave(g, c, raw, col, v):
            t = pool.tile([P, N, 4], BF16, name="grp_%d_%d" % (g, c), align_bytes=64)
            grouped[g, c] = t
            if v < N:
                nc.scalar.copy(
                    out=t[:, v:N, :].rearrange("p (c i) j -> p c j i", i=4),
                    in_=raw[:, :, col + v : col + N].rearrange("p j (c i) -> p c j i", i=4),
                )
            if v > 0:
                nc.vector.tensor_copy(
                    out=t[:, 0:v, :].rearrange("p (c i) j -> p c j i", i=4),
                    in_=raw[:, :, col : col + v].rearrange("p j (c i) -> p c j i", i=4),
                )

        def quantize(g, c):
            k = pool.tile([P, N], U32, name="cod_%d_%d" % (g, c), align_bytes=64)
            s = pool.tile([P, N], U8, name="sca_%d_%d" % (g, c), align_bytes=64)
            nc.vector.quantize_mx(
                out=k[:].bitcast(E5M2), scales=s[:], in_=grouped[g, c][:].rearrange("p h j -> p (h j)")
            )
            codes[g, c], scales[g, c] = k, s

        def multiply(g, c, start, stop):
            for m in range(2):
                if g == 2:
                    lhsT = x8_codes[:, P * m : P * (m + 1)].bitcast(E4M3)
                    lhsT_scale = x8_scales[:, P * m : P * (m + 1)]
                else:
                    lhsT = x4_wd[:, g, 2 * P * m : 2 * P * (m + 1)].bitcast(E2M1)
                    lhsT_scale = x4_sc[:, g, P * m : P * (m + 1)]
                nc.tensor.matmul_mx(
                    out=acc[c, m][:],
                    lhsT=lhsT,
                    lhsT_scale=lhsT_scale,
                    rhs=codes[g, c][:].bitcast(E5M2),
                    rhs_scale=scales[g, c][:],
                    start=start,
                    stop=stop,
                )

        def finish(c, m, parts=1):
            width = N // parts
            for i in range(parts):
                cols = slice(width * i, width * (i + 1))
                o = pool.tile([P, width], F32, name="o_%d_%d_%d" % (c, m, i), align_bytes=64)
                nc.vector.scalar_tensor_tensor(
                    out=o[:], in0=acc[c, m][:, cols], scalar=-0.0625, in1=w_sb[c, m][:, cols], op0=MULT, op1=ADD
                )
                h0 = N * c + width * i
                nc.sync.dma_start(out=out[P * m : P * (m + 1), h0 : h0 + width], in_=o[:])

        x8_grp = pool.tile([P, D, 4], BF16, name="x8_grp", align_bytes=64)
        nc.scalar.copy(out=x8_grp[:], in_=x8_raw[:].rearrange("p j d -> p d j"))
        x8_codes = pool.tile([P, D], U32, name="x8_codes", align_bytes=64)
        x8_scales = pool.tile([P, D], U8, name="x8_scales", align_bytes=64)
        nc.vector.quantize_mx(
            out=x8_codes[:].bitcast(E4M3), scales=x8_scales[:], in_=x8_grp[:].rearrange("p d j -> p (d j)")
        )

        for g, raw, start in ((2, raw2, True), (0, raw0, False)):
            interleave(g, 0, raw, 0, 256)
            interleave(g, 1, raw, N, 256)
            quantize(g, 0)
            multiply(g, 0, start, False)
            interleave(g, 2, raw, 2 * N, 256)
            quantize(g, 1)
            multiply(g, 1, start, False)
            quantize(g, 2)
            multiply(g, 2, start, False)

        interleave(1, 0, raw1a, 0, 512)
        interleave(1, 1, raw1a, N, 32)
        quantize(1, 0)
        multiply(1, 0, False, True)
        quantize(1, 1)
        multiply(1, 1, False, True)
        interleave(1, 2, raw1b, 0, 128)
        finish(0, 0)
        finish(0, 1)
        quantize(1, 2)
        multiply(1, 2, False, True)
        finish(1, 0)
        finish(1, 1)
        finish(2, 0)
        finish(2, 1, parts=2)
